import numpy as np
import ml_dtypes


def mxq(x, axis, fmt="e4m3"):
    dtype, down = {"e4m3": (ml_dtypes.float8_e4m3fn, 7), "e5m2": (ml_dtypes.float8_e5m2, 14)}[fmt]
    v = np.moveaxis(np.asarray(x, np.float32).astype(ml_dtypes.bfloat16).astype(np.float64), axis, -1)
    blocks = v.reshape(v.shape[:-1] + (-1, 32))
    amax = np.abs(blocks).max(-1, keepdims=True)
    byte = np.maximum(np.where(amax > 0, np.frexp(amax)[1] - 1 + 127, 0) - down, 1)
    scale = np.exp2(byte - 127.0)
    codes = (blocks / scale).astype(np.float32).astype(dtype).astype(np.float64)
    return np.moveaxis((codes * scale).reshape(v.shape), -1, axis)


WIDE = False


def mx_kscale(k):
    if not WIDE:
        return np.ones(k)
    levels = np.array([10, -10, 5, -5, 0])
    if k % 512:
        return np.exp2(np.random.permutation(np.resize(levels, k // 32))).repeat(32)
    a = np.empty((k // 512, 16))
    for p in range(k // 512):
        a[p, :8] = np.random.permutation(np.resize(levels, 8))
        for g in range(8):
            far = levels[np.abs(levels - a[p, g]) >= 10]
            a[p, g + 8] = far[np.random.randint(len(far))]
    return np.exp2(a.ravel()).repeat(32)


def f64(x):
    return np.asarray(x).astype(np.float64)


def striped(idx):
    return np.tile(idx.reshape(-1, 16).T, (8, 1)).astype(np.uint16)


def unstriped(offs):
    return offs[:16].T.reshape(-1).astype(np.int64)


def striped8(idx):
    return np.concatenate([x.reshape(-1, 16).T for x in idx]).astype(np.uint16)


def runs(offs, k):
    lists = np.stack([offs[16 * r : 16 * r + 16].T.reshape(-1) for r in range(8)]).astype(np.int64)
    return lists[np.arange(k) % 512 // 64]


def pack_weight(w):
    k, n = w.shape
    w = f64(np.asarray(w, np.float32).astype(ml_dtypes.bfloat16)).reshape(k // 32, 32, n)
    amax = np.abs(w).max(1)
    byte = np.clip(np.where(amax > 0, np.frexp(amax)[1] - 1 + 127 - 7, 1), 1, 254)
    scaled = (w * np.exp2(127.0 - byte)[:, None, :]).reshape(k, n).astype(np.float32)
    words = np.ascontiguousarray(scaled.reshape(k // 512, 128, 4, n).transpose(0, 1, 3, 2)).astype(ml_dtypes.float8_e4m3fn).view(np.uint8)
    return words, np.ascontiguousarray(byte.astype(np.uint8).reshape(k // 512, 16, n))


def unpack_weight(words, scales):
    g, p, n, _ = words.shape
    vals = np.ascontiguousarray(words).view(ml_dtypes.float8_e4m3fn).astype(np.float64) * np.repeat(np.exp2(scales.astype(np.float64) - 127.0), 8, axis=1)[..., None]
    return vals.transpose(0, 1, 3, 2).reshape(g * 512, n)


E2M1 = np.array([0.0, 0.5, 1.0, 1.5, 2.0, 3.0, 4.0, 6.0, -0.0, -0.5, -1.0, -1.5, -2.0, -3.0, -4.0, -6.0])


def pack_fp4(w):
    k, n = w.shape
    w = f64(np.asarray(w, np.float32).astype(ml_dtypes.bfloat16)).reshape(k // 32, 32, n)
    amax = np.abs(w).max(1)
    mant, ex = np.frexp(amax / 6.0)
    byte = np.clip(np.where(amax > 0, np.where(mant > 0.5, ex, ex - 1) + 127, 1), 1, 254)
    scaled = (w * np.exp2(127.0 - byte)[:, None, :]).reshape(k, n).astype(np.float32)
    c = np.ascontiguousarray(scaled.reshape(k // 512, 128, 4, n).transpose(0, 1, 3, 2)).astype(ml_dtypes.float4_e2m1fn).view(np.uint8) & 0xF
    words = (c[..., 0::2] | (c[..., 1::2] << 4)).reshape(k // 512, 128, 2 * n)
    return np.ascontiguousarray(words), np.ascontiguousarray(byte.astype(np.uint8).reshape(k // 512, 16, n))


def unpack_fp4(words, scales):
    g, _, n = scales.shape
    words = np.ascontiguousarray(words).reshape(g, 128, n, 2)
    nib = np.empty((g, 128, n, 4), np.uint8)
    nib[..., 0::2] = words & 0xF
    nib[..., 1::2] = words >> 4
    vals = E2M1[nib] * np.repeat(np.exp2(scales.astype(np.float64) - 127.0), 8, axis=1)[..., None]
    return vals.transpose(0, 1, 3, 2).reshape(g * 512, n)


def sigmoid(v):
    return 1.0 / (1.0 + np.exp(-np.maximum(v, -700.0)))


K, T, S, H, C, U = 512, 2048, 512, 512, 512, 1024


def setup_inputs():
    n = np.random.standard_normal
    s = mx_kscale(K)[:, None]
    packed_xT = pack_weight(n((K, T)) * s)
    packed_w1 = pack_fp4(n((K, H)) / np.sqrt(2 * K) / s)
    packed_w2 = pack_fp4(n((K, H)) / np.sqrt(2 * K) / s)
    perm = np.stack([np.random.permutation(U) for _ in range(8)])
    return {
        "x_words": packed_xT[0],
        "x_scales": packed_xT[1],
        "w1_words": packed_w1[0],
        "w1_scales": packed_w1[1],
        "w2_words": packed_w2[0],
        "w2_scales": packed_w2[1],
        "sl": np.random.uniform(1.0, 2.0, (H, 1)).astype(np.float32),
        "th": (0.5 * n((H, 1))).astype(np.float32),
        "gs": (np.random.uniform(0.5, 1.5, (K, 1)) / s).astype(np.float32),
        "offs": striped(np.random.permutation(T)[:S]),
        "hz": striped8(np.random.randint(0, T, (8, S))),
        "n1": striped8(np.stack([np.random.permutation(S) for _ in range(8)])),
        "n2": striped8(np.stack([np.random.permutation(S) for _ in range(8)])),
        "cand": striped(np.random.permutation(T)[:C]),
        "n3": striped8(perm[:, :S]),
        "n4": striped8(perm[:, S:]),
        "n5": striped8(np.stack([np.random.permutation(U) for _ in range(8)])),
    }


def reference(x_words, x_scales, w1_words, w1_scales, w2_words, w2_scales, sl, th, gs, offs, hz, n1, n2, cand, n3, n4, n5):
    x_cand = unpack_weight(x_words, x_scales)[:, unstriped(cand)]
    xq = unpack_weight(x_words, x_scales)[:, unstriped(offs)]
    x_hz = unpack_weight(x_words, x_scales)[np.arange(K)[:, None], runs(hz, K)]
    y = unpack_fp4(w1_words, w1_scales).T @ xq + unpack_fp4(w2_words, w2_scales).T @ x_hz
    st = np.maximum(y, y[np.arange(H)[:, None], runs(n1, H)])
    sg = sigmoid(f64(sl) * (st[np.arange(H)[:, None], runs(n2, H)] - f64(th)))
    z = f64(gs) * (st * sg)
    s = 0.0625 * ((x_cand.T @ mxq(z, 0, "e4m3")))
    nw = 0.5 * s
    ph = np.zeros((C, U))
    ph[np.arange(C)[:, None], runs(n3, C)] = s
    pg = ph.copy()
    pg[np.arange(C)[:, None], runs(n4, C)] = nw
    return pg - (pg[np.arange(C)[:, None], runs(n5, C)])

@@ -1,0 +1,227 @@
+from contextlib import ExitStack
+
+import concourse.mybir as mybir
+
+F32 = mybir.dt.float32
+BF16 = mybir.dt.bfloat16
+I32 = mybir.dt.int32
+U32 = mybir.dt.uint32
+U16 = mybir.dt.uint16
+U8 = mybir.dt.uint8
+FP8X4 = mybir.dt.float8_e4m3fn_x4
+FP4X4 = mybir.dt.float4_e2m1fn_x4
+ACT = mybir.ActivationFunctionType
+ALU = mybir.AluOpType
+
+P = 128
+PACK = 4
+T, S, U = 2048, 512, 1024
+FLOPS = 3 * 2 * 512 * 512 * 512
+HEAD = 128
+
+
+def tile_picked_thcehhpagtwo_none_p_kernel(
+    tc, x_words, x_scales, w1_words, w1_scales, w2_words, w2_scales, sl, th, gs,
+    offs, hz, n1, n2, cand, n3, n4, n5, out,
+):
+    nc = tc.nc
+    with ExitStack() as ctx:
+        lists = ctx.enter_context(tc.tile_pool(name="lists", bufs=1))
+        sb = ctx.enter_context(tc.tile_pool(name="sb", bufs=1))
+        ps = ctx.enter_context(tc.psum_pool(name="ps", bufs=1))
+
+        def new(shape, dtype, name, tag=None):
+            return sb.tile(shape, dtype, name=name, tag=tag or name, align_bytes=64)
+
+        def load_list(src, name):
+            tile = lists.tile(list(src.shape), U16, name=name)
+            nc.sync.dma_start(tile[:], src)
+            return tile
+
+        def entries(tile, a, b):
+            return tile[:, a // 16 : b // 16]
+
+        def load_scale_rows(queue, tile, src):
+            for r in range(4):
+                queue.dma_start(tile[r:P:32, :].bitcast(I32), src[0, r:16:4, :].bitcast(I32))
+
+        xs = new([P, T], U8, "xs")
+        nc.gpsimd.memset(xs[:].bitcast(I32), 0)
+        ws = [new([P, S], U8, "w%d_s" % a) for a in (1, 2)]
+        for tile in ws:
+            nc.vector.memset(tile[:].bitcast(I32), 0)
+
+        ww = [new([P, 2 * S], U8, "w%d_w" % a) for a in (1, 2)]
+        hz_l = load_list(hz, "hz_l")
+        nc.scalar.dma_start(ww[0][:].bitcast(I32), w1_words[0].bitcast(I32))
+        for r, queue in ((0, nc.sync), (1, nc.scalar)):
+            queue.dma_start(xs[r:P:16, :].bitcast(I32), x_scales[0, r:16:2, :].bitcast(I32))
+        for r, queue in ((2, nc.sync), (3, nc.scalar)):
+            queue.dma_start(xs[r:P:32, :].bitcast(I32), x_scales[0, r:16:4, :].bitcast(I32))
+        offs_l = load_list(offs, "offs_l")
+        xw = new([P, T], U32, "xw")
+        nc.scalar.dma_start(xw[:].bitcast(I32), x_words[0].rearrange("p c r -> p (c r)").bitcast(I32))
+        cand_l = load_list(cand, "cand_l")
+        load_scale_rows(nc.gpsimd, ws[0], w1_scales)
+        load_scale_rows(nc.sync, ws[1], w2_scales)
+        nc.scalar.dma_start(ww[1][:].bitcast(I32), w2_words[0].bitcast(I32))
+
+        hz_b = new([P, S], U8, "hz_b")
+        nc.vector.tensor_copy(hz_b[:], xs[:].indirect(hz_l[:]))
+        hz_s = new([P, S], U8, "hz_s")
+        nc.vector.tensor_copy(hz_s[:].bitcast(I32), hz_b[:].bitcast(I32))
+        for r in (2, 3):
+            nc.sync.dma_start(hz_s[r:P:32, :].bitcast(I32), hz_b[14 + r : P : 32, :].bitcast(I32))
+        n1_l = load_list(n1, "n1_l")
+        n2_l = load_list(n2, "n2_l")
+        rowv = [new([P, PACK], F32, nm) for nm in ("sl_t", "th_t", "gs_t")]
+        for tile, src in zip(rowv, (sl, th, gs)):
+            nc.sync.dma_start(tile[:], src.rearrange("(p t) o -> p (t o)", t=PACK))
+        sl_t, th_t, gs_t = rowv
+        n3_l = load_list(n3, "n3_l")
+        n4_l = load_list(n4, "n4_l")
+        n5_l = load_list(n5, "n5_l")
+        sl_th = new([P, PACK], F32, "sl_th")
+        nc.gpsimd.tensor_tensor(sl_th[:], sl_t[:], th_t[:], ALU.mult)
+        bias = new([P, PACK], F32, "bias")
+        nc.gpsimd.tensor_scalar(bias[:], sl_th[:], -1.0, 0.0, ALU.mult, ALU.add)
+
+        offs_s = new([P, S], U8, "offs_s")
+        nc.vector.tensor_copy(offs_s[:], xs[:].indirect(offs_l[:]))
+
+        wd = [new([P, 2 * S], U8, "w%d_wd" % a) for a in (1, 2)]
+        wsd = [new([P, S], U8, "w%d_sd" % a) for a in (1, 2)]
+        for a in range(2):
+            nc.scalar.copy(
+                wd[a][:].bitcast(U16).rearrange("p (t m) -> p t m", t=PACK),
+                ww[a][:].bitcast(U16).rearrange("p (m t) -> p t m", t=PACK),
+            )
+            nc.gpsimd.tensor_copy(
+                wsd[a][:].rearrange("p (t m) -> p t m", t=PACK), ws[a][:].rearrange("p (m t) -> p t m", t=PACK)
+            )
+        offs_w = new([P, S], U32, "offs_w")
+        nc.vector.tensor_copy(offs_w[:], xw[:].indirect(offs_l[:]))
+        hz_w = new([P, S], U32, "hz_w")
+        nc.vector.tensor_copy(hz_w[:], xw[:].indirect(hz_l[:]))
+        cand_s = new([P, S], U8, "cand_s", tag="hz_b")
+        nc.vector.tensor_copy(cand_s[:].rearrange("p (c m) -> p m c", c=PACK), xs[:].indirect(cand_l[:]))
+
+        y_ps = [ps.tile([P, S], F32, name="y_ps%d" % t, tag="bank%d" % t) for t in range(PACK)]
+        for t in range(PACK):
+            for a, (words, scales) in enumerate(((offs_w, offs_s), (hz_w, hz_s))):
+                nc.tensor.matmul_mx(
+                    y_ps[t][:],
+                    lhsT=wd[a][:, 2 * P * t : 2 * P * (t + 1)].bitcast(FP4X4),
+                    lhsT_scale=wsd[a][:, P * t : P * (t + 1)],
+                    rhs=words[:].bitcast(FP8X4),
+                    rhs_scale=scales[:],
+                    start=(a == 0),
+                    stop=(a == 1),
+                )
+
+        y = [new([P, S], F32, "y%d" % t) for t in range(PACK)]
+        y_n1 = [new([P, S], F32, "y_n1_%d" % t) for t in range(PACK)]
+        st = [new([P, S], F32, "st%d" % t) for t in range(PACK)]
+        nc.scalar.copy(y[0][:], y_ps[0][:])
+        for t in range(1, PACK):
+            nc.vector.tensor_copy(y[t][:], y_ps[t][:])
+        cand_w = new([P, S], U32, "cand_w", tag="hz_w")
+        for t in range(PACK):
+            for a in (0, S // 2):
+                b = a + S // 2
+                nc.scalar.activation(y_n1[t][:, a:b], y[t][:].indirect(entries(n1_l, a, b)), ACT.Copy)
+                nc.vector.tensor_tensor(st[t][:, a:b], y[t][:, a:b], y_n1[t][:, a:b], ALU.max)
+            if t == 0:
+                nc.vector.tensor_copy(
+                    cand_w[:].rearrange("p (c m) -> p m c", c=PACK), xw[:].indirect(cand_l[:])
+                )
+
+        s = [new([P, S], F32, "s%d" % c) for c in range(PACK)]
+        nw = [new([P, S], F32, "nw%d" % c) for c in range(PACK)]
+        pg = [new([P, U], F32, "pg%d" % c) for c in range(PACK)]
+
+        def make_planes(a, b, first_tag, late_tag):
+            n = b - a
+            sg_first = new([P, 1, n], F32, "sg_first%d" % a, tag=first_tag)
+            sg_late = new([P, PACK - 1, n], F32, "sg_late%d" % a, tag=late_tag)
+            planes = new([P, PACK, n], BF16, "planes%d" % a)
+            for t in range(PACK):
+                sg = sg_first[:, 0, :] if t == 0 else sg_late[:, t - 1, :]
+                for u in range(a, b, S // 2):
+                    v = min(u + S // 2, b)
+                    nc.scalar.activation(
+                        sg[:, u - a : v - a], st[t][:].indirect(entries(n2_l, u, v)), ACT.Sigmoid,
+                        bias=bias[:, t : t + 1], scale=sl_t[:, t : t + 1],
+                    )
+                nc.vector.scalar_tensor_tensor(
+                    planes[:, t, :], st[t][:, a:b], gs_t[:, t : t + 1], sg, ALU.mult, ALU.mult
+                )
+            return planes
+
+        def quantise(planes, a, b, weave):
+            n = b - a
+            woven = new([P, n * PACK], BF16, "woven%d" % a)
+            weave(
+                woven[:].rearrange("p (g i t) -> p g t i", i=4, t=PACK),
+                planes[:].rearrange("p t (g i) -> p g t i", i=4),
+            )
+            z_w = new([P, n], U32, "z_w%d" % a)
+            z_s = new([P, n], U8, "z_s%d" % a)
+            nc.vector.quantize_mx(z_w[:].bitcast(FP8X4), z_s[:], woven[:])
+            return z_w, z_s
+
+        def scores(c, a, b, z_w, z_s, bank):
+            acc = ps.tile([P, b - a], F32, name="s_ps%d_%d" % (a, c), tag="bank%d" % bank)
+            u = 0
+            while u < b - a:
+                v = u + (256 if b - a - u >= 256 else P)
+                nc.tensor.matmul_mx(
+                    acc[:, u:v],
+                    lhsT=cand_w[:, P * c : P * (c + 1)].bitcast(FP8X4),
+                    lhsT_scale=cand_s[:, P * c : P * (c + 1)],
+                    rhs=z_w[:, u:v].bitcast(FP8X4),
+                    rhs_scale=z_s[:, u:v],
+                    start=True,
+                    stop=True,
+                )
+                u = v
+            return acc
+
+        def place(c, acc, dst, factor, places, a, b):
+            nc.scalar.activation(dst[c][:, a:b], acc[c][:], ACT.Copy, scale=factor)
+            nc.vector.tensor_copy(pg[c][:].indirect(entries(places, a, b)), dst[c][:, a:b])
+
+        out_rows = out.rearrange("(p c) w -> c p w", c=PACK)
+
+        def finish(c):
+            far = new([P, U], F32, "far%d" % c)
+            res = new([P, U], F32, "res%d" % c)
+            step = U // 4 if c == PACK - 1 else U // 2
+            for a in range(0, U, step):
+                nc.scalar.activation(far[:, a : a + step], pg[c][:].indirect(entries(n5_l, a, a + step)), ACT.Copy)
+            step = U // 4 if c == PACK - 1 else U
+            for a in range(0, U, step):
+                nc.vector.tensor_tensor(res[:, a : a + step], pg[c][:, a : a + step], far[:, a : a + step], ALU.subtract)
+                nc.sync.dma_start(out_rows[c][:, a : a + step], res[:, a : a + step])
+
+        z_w, z_s = quantise(make_planes(0, HEAD, None, None), 0, HEAD, nc.vector.tensor_copy)
+        acc = [scores(c, 0, HEAD, z_w, z_s, PACK + c) for c in range(PACK)]
+        for c in range(PACK):
+            place(c, acc, s, 0.0625, n3_l, 0, HEAD)
+        planes = make_planes(HEAD, S, "planes0", "z_w0")
+        for c in range(PACK - 1):
+            place(c, acc, nw, 0.03125, n4_l, 0, HEAD)
+        z_w, z_s = quantise(planes, HEAD, S, nc.scalar.copy)
+        place(PACK - 1, acc, nw, 0.03125, n4_l, 0, HEAD)
+        acc = [scores(c, HEAD, S, z_w, z_s, c) for c in range(PACK)]
+        for c in (0, 1):
+            place(c, acc, s, 0.0625, n3_l, HEAD, S)
+        for c in (0, 1):
+            place(c, acc, nw, 0.03125, n4_l, HEAD, S)
+        for c in (2, 3):
+            place(c, acc, s, 0.0625, n3_l, HEAD, S)
+            finish(c - 2)
+        for c in (2, 3):
+            place(c, acc, nw, 0.03125, n4_l, HEAD, S)
+        for c in (2, 3):
+            finish(c)

@@ -59,6 +59,9 @@ def tile_picked_thcehhpagtwo_none_p_kernel(
         for r, queue in ((2, nc.sync), (3, nc.scalar)):
             queue.dma_start(xs[r:P:32, :].bitcast(I32), x_scales[0, r:16:4, :].bitcast(I32))
         offs_l = load_list(offs, "offs_l")
+        warm = new([P, 2], F32, "warm")
+        nc.vector.memset(warm[:, 0:1], 0.0)
+        nc.scalar.activation(warm[:, 1:2], warm[:, 0:1], ACT.Sigmoid)
         xw = new([P, T], U32, "xw")
         nc.scalar.dma_start(xw[:].bitcast(I32), x_words[0].rearrange("p c r -> p (c r)").bitcast(I32))
         cand_l = load_list(cand, "cand_l")

@@ -16,8 +16,13 @@ ALU = mybir.AluOpType
 P = 128
 PACK = 4
 T, S, U = 2048, 512, 1024
-FLOPS = 3 * 2 * 512 * 512 * 512
+QUAD = 32
+GROUP = 16
+SCALE_ROWS = 16
+HALF = S // 2
 HEAD = 128
+S_FACTOR, NW_FACTOR = 0.0625, 0.0625 * 0.5
+FLOPS = 3 * 2 * 512 * 512 * 512
 
 
 def tile_picked_thcehhpagtwo_none_p_kernel(
@@ -39,48 +44,55 @@ def tile_picked_thcehhpagtwo_none_p_kernel(
             return tile
 
         def entries(tile, a, b):
-            return tile[:, a // 16 : b // 16]
+            return tile[:, a // GROUP : b // GROUP]
 
         def load_scale_rows(queue, tile, src):
             for r in range(4):
-                queue.dma_start(tile[r:P:32, :].bitcast(I32), src[0, r:16:4, :].bitcast(I32))
+                queue.dma_start(tile[r:P:QUAD, :].bitcast(I32), src[0, r:SCALE_ROWS:4, :].bitcast(I32))
 
-        xs = new([P, T], U8, "xs")
-        nc.gpsimd.memset(xs[:].bitcast(I32), 0)
-        ws = [new([P, S], U8, "w%d_s" % a) for a in (1, 2)]
-        for tile in ws:
+        def dealt(ap):
+            return ap.rearrange("p (t m) -> p t m", t=PACK)
+
+        def undealt(ap):
+            return ap.rearrange("p (m t) -> p t m", t=PACK)
+
+        x_s = new([P, T], U8, "x_s")
+        nc.gpsimd.memset(x_s[:].bitcast(I32), 0)
+        w_s = [new([P, S], U8, "w%d_s" % a) for a in (1, 2)]
+        for tile in w_s:
             nc.vector.memset(tile[:].bitcast(I32), 0)
 
-        ww = [new([P, 2 * S], U8, "w%d_w" % a) for a in (1, 2)]
+        w_w = [new([P, 2 * S], U8, "w%d_w" % a) for a in (1, 2)]
         hz_l = load_list(hz, "hz_l")
-        nc.scalar.dma_start(ww[0][:].bitcast(I32), w1_words[0].bitcast(I32))
+        nc.scalar.dma_start(w_w[0][:].bitcast(I32), w1_words[0].bitcast(I32))
         for r, queue in ((0, nc.sync), (1, nc.scalar)):
-            queue.dma_start(xs[r:P:16, :].bitcast(I32), x_scales[0, r:16:2, :].bitcast(I32))
+            queue.dma_start(x_s[r:P:GROUP, :].bitcast(I32), x_scales[0, r:SCALE_ROWS:2, :].bitcast(I32))
         for r, queue in ((2, nc.sync), (3, nc.scalar)):
-            queue.dma_start(xs[r:P:32, :].bitcast(I32), x_scales[0, r:16:4, :].bitcast(I32))
+            queue.dma_start(x_s[r:P:QUAD, :].bitcast(I32), x_scales[0, r:SCALE_ROWS:4, :].bitcast(I32))
         offs_l = load_list(offs, "offs_l")
         warm = new([P, 2], F32, "warm")
         nc.vector.memset(warm[:, 0:1], 0.0)
         nc.scalar.activation(warm[:, 1:2], warm[:, 0:1], ACT.Sigmoid)
-        xw = new([P, T], U32, "xw")
-        nc.scalar.dma_start(xw[:].bitcast(I32), x_words[0].rearrange("p c r -> p (c r)").bitcast(I32))
+        x_w = new([P, T], U32, "x_w")
+        nc.scalar.dma_start(x_w[:].bitcast(I32), x_words[0].rearrange("p c r -> p (c r)").bitcast(I32))
         cand_l = load_list(cand, "cand_l")
-        load_scale_rows(nc.gpsimd, ws[0], w1_scales)
-        load_scale_rows(nc.sync, ws[1], w2_scales)
-        nc.scalar.dma_start(ww[1][:].bitcast(I32), w2_words[0].bitcast(I32))
+        load_scale_rows(nc.gpsimd, w_s[0], w1_scales)
+        load_scale_rows(nc.sync, w_s[1], w2_scales)
+        nc.scalar.dma_start(w_w[1][:].bitcast(I32), w2_words[0].bitcast(I32))
 
-        hz_b = new([P, S], U8, "hz_b")
-        nc.vector.tensor_copy(hz_b[:], xs[:].indirect(hz_l[:]))
+        hz_gathered_s = new([P, S], U8, "hz_gathered_s")
+        nc.vector.tensor_copy(hz_gathered_s[:], x_s[:].indirect(hz_l[:]))
         hz_s = new([P, S], U8, "hz_s")
-        nc.vector.tensor_copy(hz_s[:].bitcast(I32), hz_b[:].bitcast(I32))
+        nc.vector.tensor_copy(hz_s[:].bitcast(I32), hz_gathered_s[:].bitcast(I32))
         for r in (2, 3):
-            nc.sync.dma_start(hz_s[r:P:32, :].bitcast(I32), hz_b[14 + r : P : 32, :].bitcast(I32))
+            nc.sync.dma_start(hz_s[r:P:QUAD, :].bitcast(I32), hz_gathered_s[GROUP + r - 2 : P : QUAD, :].bitcast(I32))
+
         n1_l = load_list(n1, "n1_l")
         n2_l = load_list(n2, "n2_l")
-        rowv = [new([P, PACK], F32, nm) for nm in ("sl_t", "th_t", "gs_t")]
-        for tile, src in zip(rowv, (sl, th, gs)):
+        row_values = [new([P, PACK], F32, name) for name in ("sl_t", "th_t", "gs_t")]
+        for tile, src in zip(row_values, (sl, th, gs)):
             nc.sync.dma_start(tile[:], src.rearrange("(p t) o -> p (t o)", t=PACK))
-        sl_t, th_t, gs_t = rowv
+        sl_t, th_t, gs_t = row_values
         n3_l = load_list(n3, "n3_l")
         n4_l = load_list(n4, "n4_l")
         n5_l = load_list(n5, "n5_l")
@@ -90,32 +102,27 @@ def tile_picked_thcehhpagtwo_none_p_kernel(
         nc.gpsimd.tensor_scalar(bias[:], sl_th[:], -1.0, 0.0, ALU.mult, ALU.add)
 
         offs_s = new([P, S], U8, "offs_s")
-        nc.vector.tensor_copy(offs_s[:], xs[:].indirect(offs_l[:]))
+        nc.vector.tensor_copy(offs_s[:], x_s[:].indirect(offs_l[:]))
 
-        wd = [new([P, 2 * S], U8, "w%d_wd" % a) for a in (1, 2)]
-        wsd = [new([P, S], U8, "w%d_sd" % a) for a in (1, 2)]
+        w_dealt_w = [new([P, 2 * S], U8, "w%d_dealt_w" % a) for a in (1, 2)]
+        w_dealt_s = [new([P, S], U8, "w%d_dealt_s" % a) for a in (1, 2)]
         for a in range(2):
-            nc.scalar.copy(
-                wd[a][:].bitcast(U16).rearrange("p (t m) -> p t m", t=PACK),
-                ww[a][:].bitcast(U16).rearrange("p (m t) -> p t m", t=PACK),
-            )
-            nc.gpsimd.tensor_copy(
-                wsd[a][:].rearrange("p (t m) -> p t m", t=PACK), ws[a][:].rearrange("p (m t) -> p t m", t=PACK)
-            )
+            nc.scalar.copy(dealt(w_dealt_w[a][:].bitcast(U16)), undealt(w_w[a][:].bitcast(U16)))
+            nc.gpsimd.tensor_copy(dealt(w_dealt_s[a][:]), undealt(w_s[a][:]))
         offs_w = new([P, S], U32, "offs_w")
-        nc.vector.tensor_copy(offs_w[:], xw[:].indirect(offs_l[:]))
+        nc.vector.tensor_copy(offs_w[:], x_w[:].indirect(offs_l[:]))
         hz_w = new([P, S], U32, "hz_w")
-        nc.vector.tensor_copy(hz_w[:], xw[:].indirect(hz_l[:]))
-        cand_s = new([P, S], U8, "cand_s", tag="hz_b")
-        nc.vector.tensor_copy(cand_s[:].rearrange("p (c m) -> p m c", c=PACK), xs[:].indirect(cand_l[:]))
+        nc.vector.tensor_copy(hz_w[:], x_w[:].indirect(hz_l[:]))
+        cand_s = new([P, S], U8, "cand_s", tag="hz_gathered_s")
+        nc.vector.tensor_copy(cand_s[:].rearrange("p (c m) -> p m c", c=PACK), x_s[:].indirect(cand_l[:]))
 
         y_ps = [ps.tile([P, S], F32, name="y_ps%d" % t, tag="bank%d" % t) for t in range(PACK)]
         for t in range(PACK):
             for a, (words, scales) in enumerate(((offs_w, offs_s), (hz_w, hz_s))):
                 nc.tensor.matmul_mx(
                     y_ps[t][:],
-                    lhsT=wd[a][:, 2 * P * t : 2 * P * (t + 1)].bitcast(FP4X4),
-                    lhsT_scale=wsd[a][:, P * t : P * (t + 1)],
+                    lhsT=w_dealt_w[a][:, 2 * P * t : 2 * P * (t + 1)].bitcast(FP4X4),
+                    lhsT_scale=w_dealt_s[a][:, P * t : P * (t + 1)],
                     rhs=words[:].bitcast(FP8X4),
                     rhs_scale=scales[:],
                     start=(a == 0),
@@ -130,43 +137,43 @@ def tile_picked_thcehhpagtwo_none_p_kernel(
             nc.vector.tensor_copy(y[t][:], y_ps[t][:])
         cand_w = new([P, S], U32, "cand_w", tag="hz_w")
         for t in range(PACK):
-            for a in (0, S // 2):
-                b = a + S // 2
+            for a in (0, HALF):
+                b = a + HALF
                 nc.scalar.activation(y_n1[t][:, a:b], y[t][:].indirect(entries(n1_l, a, b)), ACT.Copy)
                 nc.vector.tensor_tensor(st[t][:, a:b], y[t][:, a:b], y_n1[t][:, a:b], ALU.max)
             if t == 0:
                 nc.vector.tensor_copy(
-                    cand_w[:].rearrange("p (c m) -> p m c", c=PACK), xw[:].indirect(cand_l[:])
+                    cand_w[:].rearrange("p (c m) -> p m c", c=PACK), x_w[:].indirect(cand_l[:])
                 )
 
         s = [new([P, S], F32, "s%d" % c) for c in range(PACK)]
         nw = [new([P, S], F32, "nw%d" % c) for c in range(PACK)]
         pg = [new([P, U], F32, "pg%d" % c) for c in range(PACK)]
 
-        def make_planes(a, b, first_tag, late_tag):
+        def make_z(a, b, first_tag, later_tag):
             n = b - a
             sg_first = new([P, 1, n], F32, "sg_first%d" % a, tag=first_tag)
-            sg_late = new([P, PACK - 1, n], F32, "sg_late%d" % a, tag=late_tag)
-            planes = new([P, PACK, n], BF16, "planes%d" % a)
+            sg_later = new([P, PACK - 1, n], F32, "sg_later%d" % a, tag=later_tag)
+            z = new([P, PACK, n], BF16, "z%d" % a)
             for t in range(PACK):
-                sg = sg_first[:, 0, :] if t == 0 else sg_late[:, t - 1, :]
-                for u in range(a, b, S // 2):
-                    v = min(u + S // 2, b)
+                sg = sg_first[:, 0, :] if t == 0 else sg_later[:, t - 1, :]
+                for u in range(a, b, HALF):
+                    v = min(u + HALF, b)
                     nc.scalar.activation(
                         sg[:, u - a : v - a], st[t][:].indirect(entries(n2_l, u, v)), ACT.Sigmoid,
                         bias=bias[:, t : t + 1], scale=sl_t[:, t : t + 1],
                     )
                 nc.vector.scalar_tensor_tensor(
-                    planes[:, t, :], st[t][:, a:b], gs_t[:, t : t + 1], sg, ALU.mult, ALU.mult
+                    z[:, t, :], st[t][:, a:b], gs_t[:, t : t + 1], sg, ALU.mult, ALU.mult
                 )
-            return planes
+            return z
 
-        def quantise(planes, a, b, weave):
+        def quantise(z, a, b, weave):
             n = b - a
             woven = new([P, n * PACK], BF16, "woven%d" % a)
             weave(
                 woven[:].rearrange("p (g i t) -> p g t i", i=4, t=PACK),
-                planes[:].rearrange("p t (g i) -> p g t i", i=4),
+                z[:].rearrange("p t (g i) -> p g t i", i=4),
             )
             z_w = new([P, n], U32, "z_w%d" % a)
             z_s = new([P, n], U8, "z_s%d" % a)
@@ -175,9 +182,8 @@ def tile_picked_thcehhpagtwo_none_p_kernel(
 
         def scores(c, a, b, z_w, z_s, bank):
             acc = ps.tile([P, b - a], F32, name="s_ps%d_%d" % (a, c), tag="bank%d" % bank)
-            u = 0
-            while u < b - a:
-                v = u + (256 if b - a - u >= 256 else P)
+            for u in range(0, b - a, HALF):
+                v = min(u + HALF, b - a)
                 nc.tensor.matmul_mx(
                     acc[:, u:v],
                     lhsT=cand_w[:, P * c : P * (c + 1)].bitcast(FP8X4),
@@ -187,44 +193,57 @@ def tile_picked_thcehhpagtwo_none_p_kernel(
                     start=True,
                     stop=True,
                 )
-                u = v
             return acc
 
-        def place(c, acc, dst, factor, places, a, b):
-            nc.scalar.activation(dst[c][:, a:b], acc[c][:], ACT.Copy, scale=factor)
-            nc.vector.tensor_copy(pg[c][:].indirect(entries(places, a, b)), dst[c][:, a:b])
+        def place(c, acc, staged, factor, slots, a, b):
+            nc.scalar.activation(staged, acc[c][:], ACT.Copy, scale=factor)
+            nc.vector.tensor_copy(pg[c][:].indirect(entries(slots, a, b)), staged)
 
-        out_rows = out.rearrange("(p c) w -> c p w", c=PACK)
-
-        def finish(c):
-            far = new([P, U], F32, "far%d" % c)
-            res = new([P, U], F32, "res%d" % c)
-            step = U // 4 if c == PACK - 1 else U // 2
-            for a in range(0, U, step):
-                nc.scalar.activation(far[:, a : a + step], pg[c][:].indirect(entries(n5_l, a, a + step)), ACT.Copy)
-            step = U // 4 if c == PACK - 1 else U
-            for a in range(0, U, step):
-                nc.vector.tensor_tensor(res[:, a : a + step], pg[c][:, a : a + step], far[:, a : a + step], ALU.subtract)
-                nc.sync.dma_start(out_rows[c][:, a : a + step], res[:, a : a + step])
-
-        z_w, z_s = quantise(make_planes(0, HEAD, None, None), 0, HEAD, nc.vector.tensor_copy)
+        z_w, z_s = quantise(make_z(0, HEAD, None, None), 0, HEAD, nc.vector.tensor_copy)
         acc = [scores(c, 0, HEAD, z_w, z_s, PACK + c) for c in range(PACK)]
         for c in range(PACK):
-            place(c, acc, s, 0.0625, n3_l, 0, HEAD)
-        planes = make_planes(HEAD, S, "planes0", "z_w0")
-        for c in range(PACK - 1):
-            place(c, acc, nw, 0.03125, n4_l, 0, HEAD)
-        z_w, z_s = quantise(planes, HEAD, S, nc.scalar.copy)
-        place(PACK - 1, acc, nw, 0.03125, n4_l, 0, HEAD)
+            place(c, acc, s[c][:, 0:HEAD], S_FACTOR, n3_l, 0, HEAD)
+        z = make_z(HEAD, S, "z0", "z_w0")
+        for c in (0, 1):
+            place(c, acc, nw[c][:, 0:HEAD], NW_FACTOR, n4_l, 0, HEAD)
+        z_w, z_s = quantise(z, HEAD, S, nc.scalar.copy)
+        nw_kept = new([P, 2 * HEAD], F32, "nw_kept", tag="z%d" % HEAD)
+        for c in (2, 3):
+            place(c, acc, nw_kept[:, (c - 2) * HEAD : (c - 1) * HEAD], NW_FACTOR, n4_l, 0, HEAD)
+
         acc = [scores(c, HEAD, S, z_w, z_s, c) for c in range(PACK)]
-        for c in (0, 1):
-            place(c, acc, s, 0.0625, n3_l, HEAD, S)
-        for c in (0, 1):
-            place(c, acc, nw, 0.03125, n4_l, HEAD, S)
-        for c in (2, 3):
-            place(c, acc, s, 0.0625, n3_l, HEAD, S)
-            finish(c - 2)
-        for c in (2, 3):
-            place(c, acc, nw, 0.03125, n4_l, HEAD, S)
-        for c in (2, 3):
-            finish(c)
+
+        def place_s(c):
+            place(c, acc, s[c][:, HEAD:S], S_FACTOR, n3_l, HEAD, S)
+
+        def place_nw(c):
+            place(c, acc, nw[c][:, HEAD:S], NW_FACTOR, n4_l, HEAD, S)
+
+        last = PACK - 1
+        place_s(0)
+        for c in range(1, last):
+            place_s(c)
+            place_nw(c - 1)
+        place_nw(last - 1)
+        place_s(last)
+        place_nw(last)
+
+        out_rows = out.rearrange("(p c) w -> c p w", c=PACK)
+        pg_n5 = [new([P, U], F32, "pg_n5_%d" % c) for c in range(PACK)]
+        res = [new([P, U], F32, "res%d" % c) for c in range(last)]
+        for c in range(last):
+            for a in (0, U // 2):
+                b = a + U // 2
+                nc.scalar.activation(pg_n5[c][:, a:b], pg[c][:].indirect(entries(n5_l, a, b)), ACT.Copy)
+            nc.gpsimd.tensor_tensor(res[c][:], pg[c][:], pg_n5[c][:], ALU.subtract)
+            nc.sync.dma_start(out_rows[c], res[c][:])
+        res.append(new([P, U], F32, "res%d" % last, tag="pg_n5_%d" % (last - 1)))
+        for a in range(0, U, U // 4):
+            b = a + U // 4
+            looked_up = pg[last][:].indirect(entries(n5_l, a, b))
+            if a == 0:
+                nc.vector.tensor_copy(pg_n5[last][:, a:b], looked_up)
+            else:
+                nc.scalar.activation(pg_n5[last][:, a:b], looked_up, ACT.Copy)
+            nc.vector.tensor_tensor(res[last][:, a:b], pg[last][:, a:b], pg_n5[last][:, a:b], ALU.subtract)
+            nc.sync.dma_start(out_rows[last][:, a:b], res[last][:, a:b])

from contextlib import ExitStack

import concourse.mybir as mybir

F32 = mybir.dt.float32
BF16 = mybir.dt.bfloat16
I32 = mybir.dt.int32
U32 = mybir.dt.uint32
U16 = mybir.dt.uint16
U8 = mybir.dt.uint8
FP8X4 = mybir.dt.float8_e4m3fn_x4
FP4X4 = mybir.dt.float4_e2m1fn_x4
ACT = mybir.ActivationFunctionType
ALU = mybir.AluOpType

P = 128
PACK = 4
T, S, U = 2048, 512, 1024
QUAD = 32
GROUP = 16
SCALE_ROWS = 16
HALF = S // 2
HEAD = 128
S_FACTOR, NW_FACTOR = 0.0625, 0.0625 * 0.5
FLOPS = 3 * 2 * 512 * 512 * 512


def tile_picked_thcehhpagtwo_none_p_kernel(
    tc, x_words, x_scales, w1_words, w1_scales, w2_words, w2_scales, sl, th, gs,
    offs, hz, n1, n2, cand, n3, n4, n5, out,
):
    nc = tc.nc
    with ExitStack() as ctx:
        lists = ctx.enter_context(tc.tile_pool(name="lists", bufs=1))
        sb = ctx.enter_context(tc.tile_pool(name="sb", bufs=1))
        ps = ctx.enter_context(tc.psum_pool(name="ps", bufs=1))

        def new(shape, dtype, name, tag=None):
            return sb.tile(shape, dtype, name=name, tag=tag or name, align_bytes=64)

        def load_list(src, name):
            tile = lists.tile(list(src.shape), U16, name=name)
            nc.sync.dma_start(tile[:], src)
            return tile

        def entries(tile, a, b):
            return tile[:, a // GROUP : b // GROUP]

        def load_scale_rows(queue, tile, src):
            for r in range(4):
                queue.dma_start(tile[r:P:QUAD, :].bitcast(I32), src[0, r:SCALE_ROWS:4, :].bitcast(I32))

        def dealt(ap):
            return ap.rearrange("p (t m) -> p t m", t=PACK)

        def undealt(ap):
            return ap.rearrange("p (m t) -> p t m", t=PACK)

        x_s = new([P, T], U8, "x_s")
        nc.gpsimd.memset(x_s[:].bitcast(I32), 0)
        w_s = [new([P, S], U8, "w%d_s" % a) for a in (1, 2)]
        for tile in w_s:
            nc.vector.memset(tile[:].bitcast(I32), 0)

        w_w = [new([P, 2 * S], U8, "w%d_w" % a) for a in (1, 2)]
        hz_l = load_list(hz, "hz_l")
        nc.scalar.dma_start(w_w[0][:].bitcast(I32), w1_words[0].bitcast(I32))
        for r, queue in ((0, nc.sync), (1, nc.scalar)):
            queue.dma_start(x_s[r:P:GROUP, :].bitcast(I32), x_scales[0, r:SCALE_ROWS:2, :].bitcast(I32))
        for r, queue in ((2, nc.sync), (3, nc.scalar)):
            queue.dma_start(x_s[r:P:QUAD, :].bitcast(I32), x_scales[0, r:SCALE_ROWS:4, :].bitcast(I32))
        offs_l = load_list(offs, "offs_l")
        warm = new([P, 2], F32, "warm")
        nc.vector.memset(warm[:, 0:1], 0.0)
        nc.scalar.activation(warm[:, 1:2], warm[:, 0:1], ACT.Sigmoid)
        x_w = new([P, T], U32, "x_w")
        nc.scalar.dma_start(x_w[:].bitcast(I32), x_words[0].rearrange("p c r -> p (c r)").bitcast(I32))
        cand_l = load_list(cand, "cand_l")
        load_scale_rows(nc.gpsimd, w_s[0], w1_scales)
        load_scale_rows(nc.sync, w_s[1], w2_scales)
        nc.scalar.dma_start(w_w[1][:].bitcast(I32), w2_words[0].bitcast(I32))

        hz_gathered_s = new([P, S], U8, "hz_gathered_s")
        nc.vector.tensor_copy(hz_gathered_s[:], x_s[:].indirect(hz_l[:]))
        hz_s = new([P, S], U8, "hz_s")
        nc.vector.tensor_copy(hz_s[:].bitcast(I32), hz_gathered_s[:].bitcast(I32))
        for r in (2, 3):
            nc.sync.dma_start(hz_s[r:P:QUAD, :].bitcast(I32), hz_gathered_s[GROUP + r - 2 : P : QUAD, :].bitcast(I32))

        n1_l = load_list(n1, "n1_l")
        n2_l = load_list(n2, "n2_l")
        row_values = [new([P, PACK], F32, name) for name in ("sl_t", "th_t", "gs_t")]
        for tile, src in zip(row_values, (sl, th, gs)):
            nc.sync.dma_start(tile[:], src.rearrange("(p t) o -> p (t o)", t=PACK))
        sl_t, th_t, gs_t = row_values
        n3_l = load_list(n3, "n3_l")
        n4_l = load_list(n4, "n4_l")
        n5_l = load_list(n5, "n5_l")
        sl_th = new([P, PACK], F32, "sl_th")
        nc.gpsimd.tensor_tensor(sl_th[:], sl_t[:], th_t[:], ALU.mult)
        bias = new([P, PACK], F32, "bias")
        nc.gpsimd.tensor_scalar(bias[:], sl_th[:], -1.0, 0.0, ALU.mult, ALU.add)

        offs_s = new([P, S], U8, "offs_s")
        nc.vector.tensor_copy(offs_s[:], x_s[:].indirect(offs_l[:]))

        w_dealt_w = [new([P, 2 * S], U8, "w%d_dealt_w" % a) for a in (1, 2)]
        w_dealt_s = [new([P, S], U8, "w%d_dealt_s" % a) for a in (1, 2)]
        for a in range(2):
            nc.scalar.copy(dealt(w_dealt_w[a][:].bitcast(U16)), undealt(w_w[a][:].bitcast(U16)))
            nc.gpsimd.tensor_copy(dealt(w_dealt_s[a][:]), undealt(w_s[a][:]))
        offs_w = new([P, S], U32, "offs_w")
        nc.vector.tensor_copy(offs_w[:], x_w[:].indirect(offs_l[:]))
        hz_w = new([P, S], U32, "hz_w")
        nc.vector.tensor_copy(hz_w[:], x_w[:].indirect(hz_l[:]))
        cand_s = new([P, S], U8, "cand_s", tag="hz_gathered_s")
        nc.vector.tensor_copy(cand_s[:].rearrange("p (c m) -> p m c", c=PACK), x_s[:].indirect(cand_l[:]))

        y_ps = [ps.tile([P, S], F32, name="y_ps%d" % t, tag="bank%d" % t) for t in range(PACK)]
        for t in range(PACK):
            for a, (words, scales) in enumerate(((offs_w, offs_s), (hz_w, hz_s))):
                nc.tensor.matmul_mx(
                    y_ps[t][:],
                    lhsT=w_dealt_w[a][:, 2 * P * t : 2 * P * (t + 1)].bitcast(FP4X4),
                    lhsT_scale=w_dealt_s[a][:, P * t : P * (t + 1)],
                    rhs=words[:].bitcast(FP8X4),
                    rhs_scale=scales[:],
                    start=(a == 0),
                    stop=(a == 1),
                )

        y = [new([P, S], F32, "y%d" % t) for t in range(PACK)]
        y_n1 = [new([P, S], F32, "y_n1_%d" % t) for t in range(PACK)]
        st = [new([P, S], F32, "st%d" % t) for t in range(PACK)]
        nc.scalar.copy(y[0][:], y_ps[0][:])
        for t in range(1, PACK):
            nc.vector.tensor_copy(y[t][:], y_ps[t][:])
        cand_w = new([P, S], U32, "cand_w", tag="hz_w")
        for t in range(PACK):
            for a in (0, HALF):
                b = a + HALF
                nc.scalar.activation(y_n1[t][:, a:b], y[t][:].indirect(entries(n1_l, a, b)), ACT.Copy)
                nc.vector.tensor_tensor(st[t][:, a:b], y[t][:, a:b], y_n1[t][:, a:b], ALU.max)
            if t == 0:
                nc.vector.tensor_copy(
                    cand_w[:].rearrange("p (c m) -> p m c", c=PACK), x_w[:].indirect(cand_l[:])
                )

        s = [new([P, S], F32, "s%d" % c) for c in range(PACK)]
        nw = [new([P, S], F32, "nw%d" % c) for c in range(PACK)]
        pg = [new([P, U], F32, "pg%d" % c) for c in range(PACK)]

        def make_z(a, b, first_tag, later_tag):
            n = b - a
            sg_first = new([P, 1, n], F32, "sg_first%d" % a, tag=first_tag)
            sg_later = new([P, PACK - 1, n], F32, "sg_later%d" % a, tag=later_tag)
            z = new([P, PACK, n], BF16, "z%d" % a)
            for t in range(PACK):
                sg = sg_first[:, 0, :] if t == 0 else sg_later[:, t - 1, :]
                for u in range(a, b, HALF):
                    v = min(u + HALF, b)
                    nc.scalar.activation(
                        sg[:, u - a : v - a], st[t][:].indirect(entries(n2_l, u, v)), ACT.Sigmoid,
                        bias=bias[:, t : t + 1], scale=sl_t[:, t : t + 1],
                    )
                nc.vector.scalar_tensor_tensor(
                    z[:, t, :], st[t][:, a:b], gs_t[:, t : t + 1], sg, ALU.mult, ALU.mult
                )
            return z

        def quantise(z, a, b, weave):
            n = b - a
            woven = new([P, n * PACK], BF16, "woven%d" % a)
            weave(
                woven[:].rearrange("p (g i t) -> p g t i", i=4, t=PACK),
                z[:].rearrange("p t (g i) -> p g t i", i=4),
            )
            z_w = new([P, n], U32, "z_w%d" % a)
            z_s = new([P, n], U8, "z_s%d" % a)
            nc.vector.quantize_mx(z_w[:].bitcast(FP8X4), z_s[:], woven[:])
            return z_w, z_s

        def scores(c, a, b, z_w, z_s, bank):
            acc = ps.tile([P, b - a], F32, name="s_ps%d_%d" % (a, c), tag="bank%d" % bank)
            for u in range(0, b - a, HALF):
                v = min(u + HALF, b - a)
                nc.tensor.matmul_mx(
                    acc[:, u:v],
                    lhsT=cand_w[:, P * c : P * (c + 1)].bitcast(FP8X4),
                    lhsT_scale=cand_s[:, P * c : P * (c + 1)],
                    rhs=z_w[:, u:v].bitcast(FP8X4),
                    rhs_scale=z_s[:, u:v],
                    start=True,
                    stop=True,
                )
            return acc

        def place(c, acc, staged, factor, slots, a, b):
            nc.scalar.activation(staged, acc[c][:], ACT.Copy, scale=factor)
            nc.vector.tensor_copy(pg[c][:].indirect(entries(slots, a, b)), staged)

        z_w, z_s = quantise(make_z(0, HEAD, None, None), 0, HEAD, nc.vector.tensor_copy)
        acc = [scores(c, 0, HEAD, z_w, z_s, PACK + c) for c in range(PACK)]
        for c in range(PACK):
            place(c, acc, s[c][:, 0:HEAD], S_FACTOR, n3_l, 0, HEAD)
        z = make_z(HEAD, S, "z0", "z_w0")
        for c in (0, 1):
            place(c, acc, nw[c][:, 0:HEAD], NW_FACTOR, n4_l, 0, HEAD)
        z_w, z_s = quantise(z, HEAD, S, nc.scalar.copy)
        nw_kept = new([P, 2 * HEAD], F32, "nw_kept", tag="z%d" % HEAD)
        for c in (2, 3):
            place(c, acc, nw_kept[:, (c - 2) * HEAD : (c - 1) * HEAD], NW_FACTOR, n4_l, 0, HEAD)

        acc = [scores(c, HEAD, S, z_w, z_s, c) for c in range(PACK)]

        def place_s(c):
            place(c, acc, s[c][:, HEAD:S], S_FACTOR, n3_l, HEAD, S)

        def place_nw(c):
            place(c, acc, nw[c][:, HEAD:S], NW_FACTOR, n4_l, HEAD, S)

        last = PACK - 1
        place_s(0)
        for c in range(1, last):
            place_s(c)
            place_nw(c - 1)
        place_nw(last - 1)
        place_s(last)
        place_nw(last)

        out_rows = out.rearrange("(p c) w -> c p w", c=PACK)
        pg_n5 = [new([P, U], F32, "pg_n5_%d" % c) for c in range(PACK)]
        res = [new([P, U], F32, "res%d" % c) for c in range(last)]
        for c in range(last):
            for a in (0, U // 2):
                b = a + U // 2
                nc.scalar.activation(pg_n5[c][:, a:b], pg[c][:].indirect(entries(n5_l, a, b)), ACT.Copy)
            nc.gpsimd.tensor_tensor(res[c][:], pg[c][:], pg_n5[c][:], ALU.subtract)
            nc.sync.dma_start(out_rows[c], res[c][:])
        res.append(new([P, U], F32, "res%d" % last, tag="pg_n5_%d" % (last - 1)))
        for a in range(0, U, U // 4):
            b = a + U // 4
            looked_up = pg[last][:].indirect(entries(n5_l, a, b))
            if a == 0:
                nc.vector.tensor_copy(pg_n5[last][:, a:b], looked_up)
            else:
                nc.scalar.activation(pg_n5[last][:, a:b], looked_up, ACT.Copy)
            nc.vector.tensor_tensor(res[last][:, a:b], pg[last][:, a:b], pg_n5[last][:, a:b], ALU.subtract)
            nc.sync.dma_start(out_rows[last][:, a:b], res[last][:, a:b])
